import numpy as np, ml_dtypes
CORES = [10,34,74,98]
N = 4
import mx_ref
NC = 128
A = np.float32(0.0125)
BF = ml_dtypes.bfloat16
def cut(t, i, w=512):
    return t[:, w * i:w * i + w]
def tile(rs):
    return np.stack(rs, axis=2).reshape(128, -1).astype(BF)
def setup_inputs(rng):
    def f(*shape):
        return mx_ref.flush((rng.standard_normal(shape, dtype=np.float32) * np.exp2(rng.integers(-2, 3, shape[:-1] + (1,)))).astype(BF))
    return {"q": f(N, 128, 4 * NC), "k": f(N, 128, 4 * 512), "v": f(N, 128, 512)}
def setup_inputs_blocks(rng):
    d = setup_inputs(rng)
    for k in ("v",): d[k] = mx_ref.spread(d[k], rng, 4)
    for k in ("q", "k"): d[k] = mx_ref.spread(d[k], rng, 1)
    return d
def setup_inputs_wide(rng):
    d = setup_inputs(rng)
    for k in ("v",): d[k] = mx_ref.flush((d[k].astype(np.float32) * np.exp2(rng.integers(-8, 9, (N, 1, 1))).astype(np.float32)).astype(BF))
    return d
def setup_inputs_sharp(rng):
    d = setup_inputs(rng); v = d["q"].astype(np.float32).reshape(N, 128, -1, 4)
    d["q"] = mx_ref.flush((v * np.exp2(rng.integers(-2, 4, (N, 1, v.shape[2], 1))).astype(np.float32)).reshape(d["q"].shape).astype(BF))
    return d
def setup_inputs_far(rng):
    d = setup_inputs(rng); d["q"] = (d["q"].astype(np.float32) * 10).astype(BF)
    return d
def setup_inputs_faroff(rng):
    d = setup_inputs(rng); v = d["k"].astype(np.float32).reshape(N, 128, -1, 4)
    d["k"] = mx_ref.flush((v + 192 * rng.standard_normal((1, 128, 1, 4), dtype=np.float32)).reshape(d["k"].shape).astype(BF))
    return d
def reference(q, k, v, own=None):
    ONE = mx_ref.quantize(np.ones((128, 512), BF))
    K = [[mx_ref.quantize(cut(k[j], b)) for b in range(4)] for j in range(N)]; V = [mx_ref.quantize(v[j]) for j in range(N)]
    Q = [mx_ref.quantize(q[i]) for i in range(N)]
    lo = np.zeros((N, N, NC), np.float32); w = lo.copy(); wlo = lo.copy(); whi = lo.copy(); p = np.zeros((N, N, 128, 4 * NC), BF); o = np.zeros((N, 128, NC), np.float32)
    S = [[[mx_ref.matmul(K[j][b], Q[i]) * A for b in range(4)] for i in range(N)] for j in range(N)]
    for j in range(N):
        lo[j] = [np.max(s, axis=(0, 1)) for s in S[j]]
    hi = np.broadcast_to(lo.max(axis=0) + 8, lo.shape).copy()
    c = lo if own is None else own["c"]
    for j in range(N):
        for i in range(N):
            p[j][i] = tile([np.exp(np.maximum(s - c[j][i], -20).astype(np.float64)).astype(np.float32) for s in S[j][i]])
    use = p if own is None else own["p"]
    for i in range(N):
        e = np.exp((c[:, i] - c[:, i].max(axis=0)).astype(np.float64)); wlo[i] = e * (1 - 4e-5); whi[i] = e * (1 + 4e-5)
        w[i] = e if own is None else own["w"][i]
        num = den = 0
        for j in range(N):
            P = mx_ref.quantize(use[j][i])
            num = num + w[i][j].astype(np.float64) * mx_ref.matmul(V[j], P); den = den + w[i][j].astype(np.float64) * mx_ref.matmul(ONE, P)
        o[i] = (num / den).astype(np.float32)
    return {"c": c, "c__lo": lo, "c__hi": hi, "p": p, "w": w, "w__lo": wlo, "w__hi": whi, "o": o}

@@ -1,0 +1,289 @@
+from concourse.bass import DstId, RemoteDMATransfer
+from concourse.mybir import dt, AluOpType, AxisListType, ActivationFunctionType as AF
+
+SCALE = 0.0125
+LW = 132
+
+SCRATCH = {
+    "qt": ("sbuf", [128, 512], "bfloat16"),
+    "kt": ("sbuf", [128, 2048], "bfloat16"),
+    "vt": ("sbuf", [128, 512], "bfloat16"),
+    "ot": ("sbuf", [128, 512], "bfloat16"),
+    "qc": ("sbuf", [128, 512], "float8_e4m3fn_x4"), "qs": ("sbuf", [128, 512], "uint8"),
+    "kc": ("sbuf", [128, 512], "float8_e4m3fn_x4"), "ks": ("sbuf", [128, 512], "uint8"),
+    "vc": ("sbuf", [128, 256], "float8_e4m3fn_x4"), "vs": ("sbuf", [128, 256], "uint8"),
+    "m20": ("sbuf", [128, 1], "float32"), "fl": ("sbuf", [128, 1], "float32"),
+    "ps": ("psum", [128, 2048], "float32"),
+    "pa": ("psum", [128, 2048], "float32"),
+    "nm": ("sbuf", [128, 4], "float32"),
+    "nc": ("sbuf", [128, 4], "float32"),
+    "e": ("sbuf", [128, 2048], "bfloat16"),
+    "x": ("sbuf", [128, 2048], "bfloat16"),
+    "pt": ("sbuf", [128, 2048], "bfloat16"),
+    "pc": ("sbuf", [128, 512], "float8_e4m3fn_x4"), "pz": ("sbuf", [128, 512], "uint8"),
+    "snd": ("sbuf", [128, 4 * LW], "float32"),
+    "land": ("sbuf", [128, 4 * LW], "float32"),
+    "negm": ("sbuf", [128, 1], "float32"), "w4": ("sbuf", [128, 4], "float32"),
+    "t0": ("sbuf", [128, 129], "float32"), "t1": ("sbuf", [128, 129], "float32"),
+    "t2": ("sbuf", [128, 129], "float32"), "t3": ("sbuf", [128, 128], "float32"),
+    "acc": ("sbuf", [128, 129], "float32"), "acc2": ("sbuf", [128, 129], "float32"),
+    "den": ("sbuf", [128, 1], "float32"), "rec": ("sbuf", [128, 1], "float32"),
+    "num": ("sbuf", [128, 128], "float32"), "y": ("sbuf", [128, 128], "float32"), "ox": ("sbuf", [128, 128], "float32"),
+}
+
+SEMAPHORES = ["dq", "dk0", "dk1", "dv", "st", "m20", "fl", "one", "oneq", "qq", "kq", "vq", "sent",
+              "negm", "w", "t0", "t1", "t2", "t3", "acc", "acc2", "den", "rec", "num", "y", "ox",
+              "ar1", "ar2", "ar3", "arc"]
+SEMAPHORES += ["qr%d" % _r for _r in range(4)]
+for _n in ("s", "nm", "nc", "ea", "eb", "c", "t", "cl", "cp", "pq", "a", "out"):
+    SEMAPHORES += ["%s_%d" % (_n, _s) for _s in range(4)]
+
+
+def rank_program(g, core, T, topo):
+    me = T.rank_of(core)
+    if me is None:
+        return
+    sem = T.sem
+    cores = T.cores
+    n = len(cores)
+    v, a, pe, sy = g.vector, g.scalar, g.tensor, g.sync
+
+    def one_hop(d):
+        return all(topo.same_plane(topo.chip(cores[i]), topo.chip(cores[(i + d) % n])) for i in range(n))
+    off = [0] + sorted(range(1, n), key=lambda d: (one_hop(d), d))
+    whose = [(me - d) % n for d in off]
+    home = [(me + d) % n for d in off]
+
+    def engines(dst):
+        m = topo.mask(core, dst)
+        return m, bin(m).count("1")
+
+    def col(buf, s, w, lo, hi):
+        return buf[:, w * s + lo:w * s + hi]
+
+    sy.dma_start(T.qt[:], T.q[:]).then_inc(sem.dq, 16)
+    for h in range(2):
+        sy.dma_start(col(T.kt, h, 1024, 0, 1024), T.k[:, 1024 * h:1024 * h + 1024]).then_inc(sem["dk%d" % h], 16)
+    sy.dma_start(T.vt[:], T.v[:]).then_inc(sem.dv, 16)
+
+    def reduce_(s):
+        v.wait_ge(sem["s_%d" % s], 1)
+        v.tensor_reduce(col(T.nm, s, 1, 0, 1), col(T.ps, s, 512, 0, 512), AxisListType.X, AluOpType.max,
+                        negate=True).then_inc(sem["nm_%d" % s], 1)
+
+    def exp_(s):
+        nc = col(T.nc, s, 1, 0, 1)
+        a.wait_ge(sem["nm_%d" % s], 1)
+        a.activation(nc, col(T.nm, s, 1, 0, 1), AF.Identity, scale=SCALE).then_inc(sem["nc_%d" % s], 1)
+        a.wait_ge(sem["nc_%d" % s], 1)
+        for h, name in enumerate(("ea_%d", "eb_%d")):
+            a.activation(col(T.e, s, 512, 256 * h, 256 * h + 256), col(T.ps, s, 512, 256 * h, 256 * h + 256), AF.Exp,
+                         bias=nc, scale=SCALE).then_inc(sem[name % s], 1)
+        a.activation(col(T.land if s == 0 else T.snd, s, LW, 129, 130), nc, AF.Identity,
+                     scale=-1.0).then_inc(sem["c_%d" % s], 1)
+
+    def blocks(groups):
+        return [(i, b) for b in groups for i in range(4)]
+
+    def src(s, i, b):
+        return T.x[32 * i:32 * i + 32, 512 * s + 128 * b:512 * s + 128 * b + 128]
+
+    def dst(s, i, b):
+        return T.pt[32 * b:32 * b + 32, 512 * s + 128 * i:512 * s + 128 * i + 128]
+
+    def turn(s, mine, theirs):
+        for t in range(4):
+            if t % 2 == 0:
+                v.wait_ge(sem[("ea_%d", "eb_%d")[t // 2] % s], 1)
+            v.transpose(T.x[:, 512 * s + t:512 * s + 512:4],
+                        col(T.e, s, 512, 128 * t, 128 * t + 128)).then_inc(sem["t_%d" % s], 1)
+        v.wait_ge(sem["t_%d" % s], 4)
+        part = col(T.x, s, 512, 128 * min(theirs), 128 * max(theirs) + 128)
+        v.tensor_scalar(part, part, T.fl[:], None, AluOpType.max).then_inc(sem["cl_%d" % s], 1)
+        for i, b in blocks(mine):
+            v.tensor_scalar(dst(s, i, b), src(s, i, b), T.fl[32 * i:32 * i + 32, 0:1], None,
+                            AluOpType.max).then_inc(sem["cp_%d" % s], 1)
+
+    def turn_act(s, theirs):
+        a.wait_ge(sem["cl_%d" % s], 1)
+        for i, b in blocks(theirs):
+            a.activation(dst(s, i, b), src(s, i, b), AF.Copy).then_inc(sem["cp_%d" % s], 1)
+
+    def quant(s):
+        v.wait_ge(sem["cp_%d" % s], 16)
+        v.quantize_mx(col(T.pc, s, 128, 0, 128), col(T.pz, s, 128, 0, 128),
+                      col(T.pt, s, 512, 0, 512)).then_inc(sem["pq_%d" % s], 1)
+
+    def scores(s):
+        r = whose[s]
+        pe.matmul_mx(col(T.ps, s, 512, 0, 512), col(T.qc, r, 128, 0, 128), col(T.qs, r, 128, 0, 128), T.kc[:], T.ks[:],
+                     True, True).then_inc(sem["s_%d" % s], 1)
+
+    def values(s):
+        pe.wait_ge(sem["pq_%d" % s], 1)
+        pe.matmul_mx(col(T.pa, s, 512, 0, 256), col(T.pc, s, 128, 0, 128), col(T.pz, s, 128, 0, 128), T.vc[:], T.vs[:],
+                     True, True).then_inc(sem["a_%d" % s], 1)
+
+    def out(s):
+        a.wait_ge(sem["a_%d" % s], 1)
+        a.activation(col(T.snd, s, LW, 0, 129), col(T.pa, s, 512, 0, 129), AF.Copy).then_inc(sem["out_%d" % s], 1)
+
+    split = ((0, 1, 2), (3,))
+    even = ((0, 1), (2, 3))
+
+    pe.wait_ge(sem.qq, 1)
+    pe.wait_ge(sem.kq, 2)
+    scores(0)
+    for s in (1, 2, 3):
+        pe.wait_ge(sem["qr%d" % whose[s]], 2 * engines(cores[whose[s]])[1])
+        scores(s)
+    pe.wait_ge(sem.vq, 1)
+    pe.wait_ge(sem.oneq, 1)
+    for s in (1, 2, 3, 0):
+        values(s)
+
+    v.memset(T.m20[:], -20.0).then_inc(sem.m20, 1)
+    v.memset(T.ot[:], 1.0).then_inc(sem.one, 1)
+    v.wait_ge(sem.one, 1)
+    v.quantize_mx(col(T.vc, 1, 128, 0, 128), col(T.vs, 1, 128, 0, 128), T.ot[:]).then_inc(sem.oneq, 1)
+    v.wait_ge(sem.dq, 16)
+    v.quantize_mx(col(T.qc, me, 128, 0, 128), col(T.qs, me, 128, 0, 128), T.qt[:]).then_inc(sem.qq, 1)
+    for h in range(2):
+        v.wait_ge(sem["dk%d" % h], 16)
+        v.quantize_mx(col(T.kc, h, 256, 0, 256), col(T.ks, h, 256, 0, 256),
+                      col(T.kt, h, 1024, 0, 1024)).then_inc(sem.kq, 1)
+    reduce_(0)
+    v.wait_ge(sem.dv, 16)
+    v.quantize_mx(col(T.vc, 0, 128, 0, 128), col(T.vs, 0, 128, 0, 128), T.vt[:]).then_inc(sem.vq, 1)
+    v.wait_ge(sem.fl, 1)
+    reduce_(1)
+    reduce_(2)
+    turn(1, *split)
+    quant(1)
+    reduce_(3)
+    turn(2, *split)
+    quant(2)
+    turn(3, *split)
+    quant(3)
+    turn(0, *even)
+    quant(0)
+    v.wait_ge(sem.c_0, 1)
+    for s in (1, 2):
+        v.wait_ge(sem["ar%d" % s], engines(cores[home[s]])[1])
+    v.wait_ge(sem.arc, engines(cores[home[3]])[1])
+    v.tensor_reduce(T.negm[:], T.land[:, 129:4 * LW:LW], AxisListType.X, AluOpType.max, negate=True).then_inc(sem.negm, 1)
+    v.wait_ge(sem.w, 1)
+    v.tensor_scalar(T.t2[:], col(T.land, 2, LW, 0, 129), T.w4[:, 2:3], None, AluOpType.mult).then_inc(sem.t2, 1)
+    v.wait_ge(sem.t1, 1)
+    v.wait_ge(sem.t2, 1)
+    v.tensor_tensor(T.acc[:], T.t1[:], T.t2[:], AluOpType.add).then_inc(sem.acc, 1)
+    v.wait_ge(sem.t0, 1)
+    v.wait_ge(sem.acc, 1)
+    v.tensor_tensor(T.acc2[:], T.acc[:], T.t0[:], AluOpType.add).then_inc(sem.acc2, 1)
+    v.wait_ge(sem.acc2, 1)
+    v.wait_ge(sem.ar3, engines(cores[home[3]])[1])
+    v.tensor_scalar(T.den[:], col(T.land, 3, LW, 128, 129), T.w4[:, 3:4], T.acc2[:, 128:129],
+                    AluOpType.mult, AluOpType.add).then_inc(sem.den, 1)
+    v.wait_ge(sem.den, 1)
+    v.reciprocal(T.rec[:], T.den[:]).then_inc(sem.rec, 1)
+    v.wait_ge(sem.t3, 1)
+    v.tensor_tensor(T.num[:], T.acc2[:, 0:128], T.t3[:], AluOpType.add).then_inc(sem.num, 1)
+    v.wait_ge(sem.rec, 1)
+    v.wait_ge(sem.num, 1)
+
+    def norm(i, b):
+        return (T.y[32 * b:32 * b + 32, 32 * i:32 * i + 32], T.num[32 * i:32 * i + 32, 32 * b:32 * b + 32],
+                T.rec[32 * i:32 * i + 32, 0:1])
+    for i, b in blocks(even[0]):
+        y, num, rec = norm(i, b)
+        v.tensor_scalar(y, num, rec, None, AluOpType.mult).then_inc(sem.y, 1)
+    v.wait_ge(sem.y, 16)
+    v.transpose(T.ox[:], T.y[:]).then_inc(sem.ox, 1)
+
+    a.wait_ge(sem.m20, 1)
+    a.activation(T.fl[:], T.m20[:], AF.Exp).then_inc(sem.fl, 1)
+    exp_(0)
+    exp_(1)
+    exp_(2)
+    turn_act(1, split[1])
+    out(1)
+    exp_(3)
+    turn_act(2, split[1])
+    out(2)
+    turn_act(3, split[1])
+    out(3)
+    turn_act(0, even[1])
+    a.wait_ge(sem.negm, 1)
+    a.activation(T.w4[:], T.land[:, 129:4 * LW:LW], AF.Exp, bias=T.negm[:]).then_inc(sem.w, 1)
+    a.wait_ge(sem.w, 1)
+    a.wait_ge(sem.ar1, engines(cores[home[1]])[1])
+    a.activation(T.t1[:], col(T.land, 1, LW, 0, 129), AF.Identity, scale=T.w4[:, 1:2]).then_inc(sem.t1, 1)
+    a.wait_ge(sem.a_0, 1)
+    a.activation(T.t0[:], T.pa[:, 0:129], AF.Identity, scale=T.w4[:, 0:1]).then_inc(sem.t0, 1)
+    a.wait_ge(sem.ar3, engines(cores[home[3]])[1])
+    a.activation(T.t3[:], col(T.land, 3, LW, 0, 128), AF.Identity, scale=T.w4[:, 3:4]).then_inc(sem.t3, 1)
+    a.wait_ge(sem.rec, 1)
+    a.wait_ge(sem.num, 1)
+    for i, b in blocks(even[1]):
+        y, num, rec = norm(i, b)
+        a.activation(y, num, AF.Identity, scale=rec).then_inc(sem.y, 1)
+
+    sent = 0
+    g.wait_ge(sem.qq, 1)
+    mask = engines(cores[home[1]])[0] & engines(cores[home[2]])[0] & engines(cores[home[3]])[0]
+    ids = []
+    for s in (1, 2, 3):
+        rid, pid, _ = topo.addr(cores[home[s]])
+        ids.append(DstId(rid=rid, pnc=pid))
+    qs, qc = col(T.qs, me, 128, 0, 128), col(T.qc, me, 128, 0, 128).bitcast(dt.uint8)
+    g.remote_dma_fused([RemoteDMATransfer(dst_ids=ids, dma_engine_mask=mask, remote_sem=sem["qr%d" % me],
+                                          srcs=[qs], dsts=[qs] * 3)], local_sem=sem.sent)
+    sent += bin(mask).count("1")
+
+    def send(to, out_ap, in_ap, rsem):
+        m, k = engines(to)
+        rid, pid, _ = topo.addr(to)
+        g.remote_dma(out_ap, in_ap, rsem, sem.sent, pid, rid, m)
+        return k
+
+    def result(s, lo, hi, rsem):
+        return send(cores[whose[s]], col(T.land, s, LW, lo, hi), col(T.snd, s, LW, lo, hi), rsem)
+    for s in (1, 2, 3):
+        sent += send(cores[home[s]], qc, qc, sem["qr%d" % me])
+    g.wait_ge(sem.c_1, 1)
+    g.wait_ge(sem.out_1, 1)
+    sent += result(1, 0, 130, sem.ar1)
+    g.wait_ge(sem.c_3, 1)
+    sent += result(3, 129, 130, sem.arc)
+    g.wait_ge(sem.c_2, 1)
+    g.wait_ge(sem.out_2, 1)
+    sent += result(2, 0, 130, sem.ar2)
+    g.wait_ge(sem.out_3, 1)
+    sent += result(3, 0, 129, sem.ar3)
+    g.wait_ge(sem.sent, sent)
+
+    stores = 0
+
+    def store(to, what):
+        sy.dma_start(to, what).then_inc(sem.st, 16)
+        return 16
+
+    def store_c(s):
+        sy.wait_ge(sem["c_%d" % s], 1)
+        return store(T.c[whose[s]:whose[s] + 1, :], col(T.land if s == 0 else T.snd, s, LW, 129, 130))
+
+    def store_p(s):
+        sy.wait_ge(sem["cp_%d" % s], 16)
+        return store(T.p[whose[s]], col(T.pt, s, 512, 0, 512))
+    for s in (0, 1, 2):
+        stores += store_c(s)
+    stores += store_p(1)
+    stores += store_c(3)
+    for s in (2, 3, 0):
+        stores += store_p(s)
+    sy.wait_ge(sem.w, 1)
+    for s in range(4):
+        stores += store(T.w[home[s]:home[s] + 1, :], T.w4[:, s:s + 1])
+    sy.wait_ge(sem.ox, 1)
+    stores += store(T.o[:], T.ox[:])
+    sy.wait_ge(sem.st, stores)

@@ -1,8 +1,12 @@
-from concourse.bass import DstId, RemoteDMATransfer
+import math
 from concourse.mybir import dt, AluOpType, AxisListType, ActivationFunctionType as AF
 
 SCALE = 0.0125
+FLOOR = math.exp(-20.0)
 LW = 132
+TWO = (0, 1)
+SHARE = 6
+TAIL = 9
 
 SCRATCH = {
     "qt": ("sbuf", [128, 512], "bfloat16"),
@@ -12,10 +16,10 @@ SCRATCH = {
     "qc": ("sbuf", [128, 512], "float8_e4m3fn_x4"), "qs": ("sbuf", [128, 512], "uint8"),
     "kc": ("sbuf", [128, 512], "float8_e4m3fn_x4"), "ks": ("sbuf", [128, 512], "uint8"),
     "vc": ("sbuf", [128, 256], "float8_e4m3fn_x4"), "vs": ("sbuf", [128, 256], "uint8"),
-    "m20": ("sbuf", [128, 1], "float32"), "fl": ("sbuf", [128, 1], "float32"),
-    "ps": ("psum", [128, 2048], "float32"),
-    "pa": ("psum", [128, 2048], "float32"),
-    "nm": ("sbuf", [128, 4], "float32"),
+    "m20": ("sbuf", [128, 1], "float32"), "fl": ("sbuf", [128, 1], "bfloat16"),
+    "ps": ("psum", [128, 4096], "float32"),
+    "hf": ("sbuf", [128, 1024], "float32"),
+    "mx": ("sbuf", [128, 1024], "float32"),
     "nc": ("sbuf", [128, 4], "float32"),
     "e": ("sbuf", [128, 2048], "bfloat16"),
     "x": ("sbuf", [128, 2048], "bfloat16"),
@@ -35,7 +39,7 @@ SEMAPHORES = ["dq", "dk0", "dk1", "dv", "st", "m20", "fl", "one", "oneq", "qq", 
               "negm", "w", "t0", "t1", "t2", "t3", "acc", "acc2", "den", "rec", "num", "y", "ox",
               "ar1", "ar2", "ar3", "arc"]
 SEMAPHORES += ["qr%d" % _r for _r in range(4)]
-for _n in ("s", "nm", "nc", "ea", "eb", "c", "t", "cl", "cp", "pq", "a", "out"):
+for _n in ("s0", "s1", "hf", "mx", "nc", "e0", "e1", "c", "t", "cl", "cp", "pq", "a", "out"):
     SEMAPHORES += ["%s_%d" % (_n, _s) for _s in range(4)]
 
 
@@ -61,29 +65,51 @@ def rank_program(g, core, T, topo):
     def col(buf, s, w, lo, hi):
         return buf[:, w * s + lo:w * s + hi]
 
+    def bank(s, h, lo, hi):
+        return col(T.ps, s, 1024, 512 * h + lo, 512 * h + hi)
+
     sy.dma_start(T.qt[:], T.q[:]).then_inc(sem.dq, 16)
     for h in range(2):
         sy.dma_start(col(T.kt, h, 1024, 0, 1024), T.k[:, 1024 * h:1024 * h + 1024]).then_inc(sem["dk%d" % h], 16)
     sy.dma_start(T.vt[:], T.v[:]).then_inc(sem.dv, 16)
 
-    def reduce_(s):
-        v.wait_ge(sem["s_%d" % s], 1)
-        v.tensor_reduce(col(T.nm, s, 1, 0, 1), col(T.ps, s, 512, 0, 512), AxisListType.X, AluOpType.max,
-                        negate=True).then_inc(sem["nm_%d" % s], 1)
+    order = [(i, b) for b in range(4) for i in range(4)]
+    mine, theirs = order[:16 - SHARE], order[16 - SHARE:]
+
+    def half_(s):
+        if s in TWO:
+            return
+        a.wait_ge(sem["s0_%d" % s], 1)
+        a.activation(col(T.hf, s, 256, 0, 256), bank(s, 0, 0, 256), AF.Copy).then_inc(sem["hf_%d" % s], 1)
+
+    def max_(s):
+        if s in TWO:
+            for h in range(2):
+                v.wait_ge(sem["s%d_%d" % (h, s)], 1)
+                v.tensor_reduce(col(T.mx, s, 256, h, h + 1), bank(s, h, 0, 256), AxisListType.X,
+                                AluOpType.max).then_inc(sem["mx_%d" % s], 1)
+            v.wait_ge(sem["mx_%d" % s], 2)
+            v.tensor_scalar(col(T.nc, s, 1, 0, 1), col(T.mx, s, 256, 0, 1), col(T.mx, s, 256, 1, 2), -SCALE,
+                            AluOpType.max, AluOpType.mult).then_inc(sem["nc_%d" % s], 1)
+        else:
+            v.wait_ge(sem["s1_%d" % s], 1)
+            v.wait_ge(sem["hf_%d" % s], 1)
+            v.tensor_tensor_scan(col(T.mx, s, 256, 0, 256), bank(s, 1, 0, 256), col(T.hf, s, 256, 0, 256), -1e29,
+                                 AluOpType.max, AluOpType.max).then_inc(sem["mx_%d" % s], 1)
 
     def exp_(s):
         nc = col(T.nc, s, 1, 0, 1)
-        a.wait_ge(sem["nm_%d" % s], 1)
-        a.activation(nc, col(T.nm, s, 1, 0, 1), AF.Identity, scale=SCALE).then_inc(sem["nc_%d" % s], 1)
+        if s not in TWO:
+            a.wait_ge(sem["mx_%d" % s], 1)
+            a.activation(nc, col(T.mx, s, 256, 255, 256), AF.Identity, scale=-SCALE).then_inc(sem["nc_%d" % s], 1)
         a.wait_ge(sem["nc_%d" % s], 1)
-        for h, name in enumerate(("ea_%d", "eb_%d")):
-            a.activation(col(T.e, s, 512, 256 * h, 256 * h + 256), col(T.ps, s, 512, 256 * h, 256 * h + 256), AF.Exp,
-                         bias=nc, scale=SCALE).then_inc(sem[name % s], 1)
-        a.activation(col(T.land if s == 0 else T.snd, s, LW, 129, 130), nc, AF.Identity,
-                     scale=-1.0).then_inc(sem["c_%d" % s], 1)
+        for h in range(2):
+            a.activation(col(T.e, s, 512, 256 * h, 256 * h + 256), bank(s, h, 0, 256),
+                         AF.Exp, bias=nc, scale=SCALE).then_inc(sem["e%d_%d" % (h, s)], 1)
 
-    def blocks(groups):
-        return [(i, b) for b in groups for i in range(4)]
+    def shift(s):
+        a.activation(col(T.land if s == 0 else T.snd, s, LW, 129, 130), col(T.nc, s, 1, 0, 1), AF.Identity,
+                     scale=-1.0).then_inc(sem["c_%d" % s], 1)
 
     def src(s, i, b):
         return T.x[32 * i:32 * i + 32, 512 * s + 128 * b:512 * s + 128 * b + 128]
@@ -91,22 +117,23 @@ def rank_program(g, core, T, topo):
     def dst(s, i, b):
         return T.pt[32 * b:32 * b + 32, 512 * s + 128 * i:512 * s + 128 * i + 128]
 
-    def turn(s, mine, theirs):
+    def turn(s):
         for t in range(4):
-            if t % 2 == 0:
-                v.wait_ge(sem[("ea_%d", "eb_%d")[t // 2] % s], 1)
+            v.wait_ge(sem["e%d_%d" % (t // 2, s)], 1)
             v.transpose(T.x[:, 512 * s + t:512 * s + 512:4],
                         col(T.e, s, 512, 128 * t, 128 * t + 128)).then_inc(sem["t_%d" % s], 1)
         v.wait_ge(sem["t_%d" % s], 4)
-        part = col(T.x, s, 512, 128 * min(theirs), 128 * max(theirs) + 128)
+        part = col(T.x, s, 512, 128 * theirs[0][1], 512)
         v.tensor_scalar(part, part, T.fl[:], None, AluOpType.max).then_inc(sem["cl_%d" % s], 1)
-        for i, b in blocks(mine):
-            v.tensor_scalar(dst(s, i, b), src(s, i, b), T.fl[32 * i:32 * i + 32, 0:1], None,
-                            AluOpType.max).then_inc(sem["cp_%d" % s], 1)
 
-    def turn_act(s, theirs):
+    def place(s):
+        v.wait_ge(sem["cl_%d" % s], 1)
+        for i, b in mine:
+            v.tensor_scalar(dst(s, i, b), src(s, i, b), FLOOR, None, AluOpType.max).then_inc(sem["cp_%d" % s], 1)
+
+    def place_act(s):
         a.wait_ge(sem["cl_%d" % s], 1)
-        for i, b in blocks(theirs):
+        for i, b in theirs:
             a.activation(dst(s, i, b), src(s, i, b), AF.Copy).then_inc(sem["cp_%d" % s], 1)
 
     def quant(s):
@@ -116,20 +143,18 @@ def rank_program(g, core, T, topo):
 
     def scores(s):
         r = whose[s]
-        pe.matmul_mx(col(T.ps, s, 512, 0, 512), col(T.qc, r, 128, 0, 128), col(T.qs, r, 128, 0, 128), T.kc[:], T.ks[:],
-                     True, True).then_inc(sem["s_%d" % s], 1)
+        for h in range(2):
+            pe.matmul_mx(bank(s, h, 0, 256), col(T.qc, r, 128, 0, 128), col(T.qs, r, 128, 0, 128),
+                         col(T.kc, h, 256, 0, 256), col(T.ks, h, 256, 0, 256), True, True).then_inc(sem["s%d_%d" % (h, s)], 1)
 
     def values(s):
         pe.wait_ge(sem["pq_%d" % s], 1)
-        pe.matmul_mx(col(T.pa, s, 512, 0, 256), col(T.pc, s, 128, 0, 128), col(T.pz, s, 128, 0, 128), T.vc[:], T.vs[:],
+        pe.matmul_mx(bank(s, 0, 0, 256), col(T.pc, s, 128, 0, 128), col(T.pz, s, 128, 0, 128), T.vc[:], T.vs[:],
                      True, True).then_inc(sem["a_%d" % s], 1)
 
     def out(s):
         a.wait_ge(sem["a_%d" % s], 1)
-        a.activation(col(T.snd, s, LW, 0, 129), col(T.pa, s, 512, 0, 129), AF.Copy).then_inc(sem["out_%d" % s], 1)
-
-    split = ((0, 1, 2), (3,))
-    even = ((0, 1), (2, 3))
+        a.activation(col(T.snd, s, LW, 0, 129), bank(s, 0, 0, 129), AF.Copy).then_inc(sem["out_%d" % s], 1)
 
     pe.wait_ge(sem.qq, 1)
     pe.wait_ge(sem.kq, 2)
@@ -152,21 +177,17 @@ def rank_program(g, core, T, topo):
         v.wait_ge(sem["dk%d" % h], 16)
         v.quantize_mx(col(T.kc, h, 256, 0, 256), col(T.ks, h, 256, 0, 256),
                       col(T.kt, h, 1024, 0, 1024)).then_inc(sem.kq, 1)
-    reduce_(0)
+    max_(0)
     v.wait_ge(sem.dv, 16)
     v.quantize_mx(col(T.vc, 0, 128, 0, 128), col(T.vs, 0, 128, 0, 128), T.vt[:]).then_inc(sem.vq, 1)
     v.wait_ge(sem.fl, 1)
-    reduce_(1)
-    reduce_(2)
-    turn(1, *split)
-    quant(1)
-    reduce_(3)
-    turn(2, *split)
-    quant(2)
-    turn(3, *split)
-    quant(3)
-    turn(0, *even)
-    quant(0)
+    max_(1)
+    for s in (1, 2, 3, 0):
+        turn(s)
+        if s in (1, 2):
+            max_(s + 1)
+        place(s)
+        quant(s)
     v.wait_ge(sem.c_0, 1)
     for s in (1, 2):
         v.wait_ge(sem["ar%d" % s], engines(cores[home[s]])[1])
@@ -194,7 +215,7 @@ def rank_program(g, core, T, topo):
     def norm(i, b):
         return (T.y[32 * b:32 * b + 32, 32 * i:32 * i + 32], T.num[32 * i:32 * i + 32, 32 * b:32 * b + 32],
                 T.rec[32 * i:32 * i + 32, 0:1])
-    for i, b in blocks(even[0]):
+    for i, b in order[:16 - TAIL]:
         y, num, rec = norm(i, b)
         v.tensor_scalar(y, num, rec, None, AluOpType.mult).then_inc(sem.y, 1)
     v.wait_ge(sem.y, 16)
@@ -203,42 +224,40 @@ def rank_program(g, core, T, topo):
     a.wait_ge(sem.m20, 1)
     a.activation(T.fl[:], T.m20[:], AF.Exp).then_inc(sem.fl, 1)
     exp_(0)
+    shift(0)
     exp_(1)
+    half_(2)
+    place_act(1)
     exp_(2)
-    turn_act(1, split[1])
+    half_(3)
+    shift(1)
     out(1)
+    place_act(2)
     exp_(3)
-    turn_act(2, split[1])
+    shift(3)
+    shift(2)
     out(2)
-    turn_act(3, split[1])
+    place_act(3)
     out(3)
-    turn_act(0, even[1])
+    place_act(0)
     a.wait_ge(sem.negm, 1)
     a.activation(T.w4[:], T.land[:, 129:4 * LW:LW], AF.Exp, bias=T.negm[:]).then_inc(sem.w, 1)
     a.wait_ge(sem.w, 1)
     a.wait_ge(sem.ar1, engines(cores[home[1]])[1])
     a.activation(T.t1[:], col(T.land, 1, LW, 0, 129), AF.Identity, scale=T.w4[:, 1:2]).then_inc(sem.t1, 1)
     a.wait_ge(sem.a_0, 1)
-    a.activation(T.t0[:], T.pa[:, 0:129], AF.Identity, scale=T.w4[:, 0:1]).then_inc(sem.t0, 1)
+    a.activation(T.t0[:], bank(0, 0, 0, 129), AF.Identity, scale=T.w4[:, 0:1]).then_inc(sem.t0, 1)
     a.wait_ge(sem.ar3, engines(cores[home[3]])[1])
     a.activation(T.t3[:], col(T.land, 3, LW, 0, 128), AF.Identity, scale=T.w4[:, 3:4]).then_inc(sem.t3, 1)
     a.wait_ge(sem.rec, 1)
     a.wait_ge(sem.num, 1)
-    for i, b in blocks(even[1]):
+    for i, b in order[16 - TAIL:]:
         y, num, rec = norm(i, b)
         a.activation(y, num, AF.Identity, scale=rec).then_inc(sem.y, 1)
 
     sent = 0
     g.wait_ge(sem.qq, 1)
-    mask = engines(cores[home[1]])[0] & engines(cores[home[2]])[0] & engines(cores[home[3]])[0]
-    ids = []
-    for s in (1, 2, 3):
-        rid, pid, _ = topo.addr(cores[home[s]])
-        ids.append(DstId(rid=rid, pnc=pid))
     qs, qc = col(T.qs, me, 128, 0, 128), col(T.qc, me, 128, 0, 128).bitcast(dt.uint8)
-    g.remote_dma_fused([RemoteDMATransfer(dst_ids=ids, dma_engine_mask=mask, remote_sem=sem["qr%d" % me],
-                                          srcs=[qs], dsts=[qs] * 3)], local_sem=sem.sent)
-    sent += bin(mask).count("1")
 
     def send(to, out_ap, in_ap, rsem):
         m, k = engines(to)
@@ -249,7 +268,8 @@ def rank_program(g, core, T, topo):
     def result(s, lo, hi, rsem):
         return send(cores[whose[s]], col(T.land, s, LW, lo, hi), col(T.snd, s, LW, lo, hi), rsem)
     for s in (1, 2, 3):
-        sent += send(cores[home[s]], qc, qc, sem["qr%d" % me])
+        for part in (qs, qc):
+            sent += send(cores[home[s]], part, part, sem["qr%d" % me])
     g.wait_ge(sem.c_1, 1)
     g.wait_ge(sem.out_1, 1)
     sent += result(1, 0, 130, sem.ar1)
@@ -275,11 +295,12 @@ def rank_program(g, core, T, topo):
     def store_p(s):
         sy.wait_ge(sem["cp_%d" % s], 16)
         return store(T.p[whose[s]], col(T.pt, s, 512, 0, 512))
-    for s in (0, 1, 2):
-        stores += store_c(s)
+    stores += store_c(0)
+    stores += store_c(1)
     stores += store_p(1)
     stores += store_c(3)
-    for s in (2, 3, 0):
+    stores += store_c(2)
+    for s in (0, 2, 3):
         stores += store_p(s)
     sy.wait_ge(sem.w, 1)
     for s in range(4):

@@ -5,8 +5,8 @@ SCALE = 0.0125
 FLOOR = math.exp(-20.0)
 LW = 132
 TWO = (0, 1)
-SHARE = 6
-TAIL = 9
+SHARE = 4
+TAIL = 7
 
 SCRATCH = {
     "qt": ("sbuf", [128, 512], "bfloat16"),
@@ -127,7 +127,6 @@ def rank_program(g, core, T, topo):
         v.tensor_scalar(part, part, T.fl[:], None, AluOpType.max).then_inc(sem["cl_%d" % s], 1)
 
     def place(s):
-        v.wait_ge(sem["cl_%d" % s], 1)
         for i, b in mine:
             v.tensor_scalar(dst(s, i, b), src(s, i, b), FLOOR, None, AluOpType.max).then_inc(sem["cp_%d" % s], 1)
 
@@ -187,6 +186,7 @@ def rank_program(g, core, T, topo):
         if s in (1, 2):
             max_(s + 1)
         place(s)
+        v.wait_ge(sem["cl_%d" % s], 1)
         quant(s)
     v.wait_ge(sem.c_0, 1)
     for s in (1, 2):

import math
from concourse.mybir import dt, AluOpType, AxisListType, ActivationFunctionType as AF

SCALE = 0.0125
FLOOR = math.exp(-20.0)
LW = 132
TWO = (0, 1)
SHARE = 4
TAIL = 7

SCRATCH = {
    "qt": ("sbuf", [128, 512], "bfloat16"),
    "kt": ("sbuf", [128, 2048], "bfloat16"),
    "vt": ("sbuf", [128, 512], "bfloat16"),
    "ot": ("sbuf", [128, 512], "bfloat16"),
    "qc": ("sbuf", [128, 512], "float8_e4m3fn_x4"), "qs": ("sbuf", [128, 512], "uint8"),
    "kc": ("sbuf", [128, 512], "float8_e4m3fn_x4"), "ks": ("sbuf", [128, 512], "uint8"),
    "vc": ("sbuf", [128, 256], "float8_e4m3fn_x4"), "vs": ("sbuf", [128, 256], "uint8"),
    "m20": ("sbuf", [128, 1], "float32"), "fl": ("sbuf", [128, 1], "bfloat16"),
    "ps": ("psum", [128, 4096], "float32"),
    "hf": ("sbuf", [128, 1024], "float32"),
    "mx": ("sbuf", [128, 1024], "float32"),
    "nc": ("sbuf", [128, 4], "float32"),
    "e": ("sbuf", [128, 2048], "bfloat16"),
    "x": ("sbuf", [128, 2048], "bfloat16"),
    "pt": ("sbuf", [128, 2048], "bfloat16"),
    "pc": ("sbuf", [128, 512], "float8_e4m3fn_x4"), "pz": ("sbuf", [128, 512], "uint8"),
    "snd": ("sbuf", [128, 4 * LW], "float32"),
    "land": ("sbuf", [128, 4 * LW], "float32"),
    "negm": ("sbuf", [128, 1], "float32"), "w4": ("sbuf", [128, 4], "float32"),
    "t0": ("sbuf", [128, 129], "float32"), "t1": ("sbuf", [128, 129], "float32"),
    "t2": ("sbuf", [128, 129], "float32"), "t3": ("sbuf", [128, 128], "float32"),
    "acc": ("sbuf", [128, 129], "float32"), "acc2": ("sbuf", [128, 129], "float32"),
    "den": ("sbuf", [128, 1], "float32"), "rec": ("sbuf", [128, 1], "float32"),
    "num": ("sbuf", [128, 128], "float32"), "y": ("sbuf", [128, 128], "float32"), "ox": ("sbuf", [128, 128], "float32"),
}

SEMAPHORES = ["dq", "dk0", "dk1", "dv", "st", "m20", "fl", "one", "oneq", "qq", "kq", "vq", "sent",
              "negm", "w", "t0", "t1", "t2", "t3", "acc", "acc2", "den", "rec", "num", "y", "ox",
              "ar1", "ar2", "ar3", "arc"]
SEMAPHORES += ["qr%d" % _r for _r in range(4)]
for _n in ("s0", "s1", "hf", "mx", "nc", "e0", "e1", "c", "t", "cl", "cp", "pq", "a", "out"):
    SEMAPHORES += ["%s_%d" % (_n, _s) for _s in range(4)]


def rank_program(g, core, T, topo):
    me = T.rank_of(core)
    if me is None:
        return
    sem = T.sem
    cores = T.cores
    n = len(cores)
    v, a, pe, sy = g.vector, g.scalar, g.tensor, g.sync

    def one_hop(d):
        return all(topo.same_plane(topo.chip(cores[i]), topo.chip(cores[(i + d) % n])) for i in range(n))
    off = [0] + sorted(range(1, n), key=lambda d: (one_hop(d), d))
    whose = [(me - d) % n for d in off]
    home = [(me + d) % n for d in off]

    def engines(dst):
        m = topo.mask(core, dst)
        return m, bin(m).count("1")

    def col(buf, s, w, lo, hi):
        return buf[:, w * s + lo:w * s + hi]

    def bank(s, h, lo, hi):
        return col(T.ps, s, 1024, 512 * h + lo, 512 * h + hi)

    sy.dma_start(T.qt[:], T.q[:]).then_inc(sem.dq, 16)
    for h in range(2):
        sy.dma_start(col(T.kt, h, 1024, 0, 1024), T.k[:, 1024 * h:1024 * h + 1024]).then_inc(sem["dk%d" % h], 16)
    sy.dma_start(T.vt[:], T.v[:]).then_inc(sem.dv, 16)

    order = [(i, b) for b in range(4) for i in range(4)]
    mine, theirs = order[:16 - SHARE], order[16 - SHARE:]

    def half_(s):
        if s in TWO:
            return
        a.wait_ge(sem["s0_%d" % s], 1)
        a.activation(col(T.hf, s, 256, 0, 256), bank(s, 0, 0, 256), AF.Copy).then_inc(sem["hf_%d" % s], 1)

    def max_(s):
        if s in TWO:
            for h in range(2):
                v.wait_ge(sem["s%d_%d" % (h, s)], 1)
                v.tensor_reduce(col(T.mx, s, 256, h, h + 1), bank(s, h, 0, 256), AxisListType.X,
                                AluOpType.max).then_inc(sem["mx_%d" % s], 1)
            v.wait_ge(sem["mx_%d" % s], 2)
            v.tensor_scalar(col(T.nc, s, 1, 0, 1), col(T.mx, s, 256, 0, 1), col(T.mx, s, 256, 1, 2), -SCALE,
                            AluOpType.max, AluOpType.mult).then_inc(sem["nc_%d" % s], 1)
        else:
            v.wait_ge(sem["s1_%d" % s], 1)
            v.wait_ge(sem["hf_%d" % s], 1)
            v.tensor_tensor_scan(col(T.mx, s, 256, 0, 256), bank(s, 1, 0, 256), col(T.hf, s, 256, 0, 256), -1e29,
                                 AluOpType.max, AluOpType.max).then_inc(sem["mx_%d" % s], 1)

    def exp_(s):
        nc = col(T.nc, s, 1, 0, 1)
        if s not in TWO:
            a.wait_ge(sem["mx_%d" % s], 1)
            a.activation(nc, col(T.mx, s, 256, 255, 256), AF.Identity, scale=-SCALE).then_inc(sem["nc_%d" % s], 1)
        a.wait_ge(sem["nc_%d" % s], 1)
        for h in range(2):
            a.activation(col(T.e, s, 512, 256 * h, 256 * h + 256), bank(s, h, 0, 256),
                         AF.Exp, bias=nc, scale=SCALE).then_inc(sem["e%d_%d" % (h, s)], 1)

    def shift(s):
        a.activation(col(T.land if s == 0 else T.snd, s, LW, 129, 130), col(T.nc, s, 1, 0, 1), AF.Identity,
                     scale=-1.0).then_inc(sem["c_%d" % s], 1)

    def src(s, i, b):
        return T.x[32 * i:32 * i + 32, 512 * s + 128 * b:512 * s + 128 * b + 128]

    def dst(s, i, b):
        return T.pt[32 * b:32 * b + 32, 512 * s + 128 * i:512 * s + 128 * i + 128]

    def turn(s):
        for t in range(4):
            v.wait_ge(sem["e%d_%d" % (t // 2, s)], 1)
            v.transpose(T.x[:, 512 * s + t:512 * s + 512:4],
                        col(T.e, s, 512, 128 * t, 128 * t + 128)).then_inc(sem["t_%d" % s], 1)
        v.wait_ge(sem["t_%d" % s], 4)
        part = col(T.x, s, 512, 128 * theirs[0][1], 512)
        v.tensor_scalar(part, part, T.fl[:], None, AluOpType.max).then_inc(sem["cl_%d" % s], 1)

    def place(s):
        for i, b in mine:
            v.tensor_scalar(dst(s, i, b), src(s, i, b), FLOOR, None, AluOpType.max).then_inc(sem["cp_%d" % s], 1)

    def place_act(s):
        a.wait_ge(sem["cl_%d" % s], 1)
        for i, b in theirs:
            a.activation(dst(s, i, b), src(s, i, b), AF.Copy).then_inc(sem["cp_%d" % s], 1)

    def quant(s):
        v.wait_ge(sem["cp_%d" % s], 16)
        v.quantize_mx(col(T.pc, s, 128, 0, 128), col(T.pz, s, 128, 0, 128),
                      col(T.pt, s, 512, 0, 512)).then_inc(sem["pq_%d" % s], 1)

    def scores(s):
        r = whose[s]
        for h in range(2):
            pe.matmul_mx(bank(s, h, 0, 256), col(T.qc, r, 128, 0, 128), col(T.qs, r, 128, 0, 128),
                         col(T.kc, h, 256, 0, 256), col(T.ks, h, 256, 0, 256), True, True).then_inc(sem["s%d_%d" % (h, s)], 1)

    def values(s):
        pe.wait_ge(sem["pq_%d" % s], 1)
        pe.matmul_mx(bank(s, 0, 0, 256), col(T.pc, s, 128, 0, 128), col(T.pz, s, 128, 0, 128), T.vc[:], T.vs[:],
                     True, True).then_inc(sem["a_%d" % s], 1)

    def out(s):
        a.wait_ge(sem["a_%d" % s], 1)
        a.activation(col(T.snd, s, LW, 0, 129), bank(s, 0, 0, 129), AF.Copy).then_inc(sem["out_%d" % s], 1)

    pe.wait_ge(sem.qq, 1)
    pe.wait_ge(sem.kq, 2)
    scores(0)
    for s in (1, 2, 3):
        pe.wait_ge(sem["qr%d" % whose[s]], 2 * engines(cores[whose[s]])[1])
        scores(s)
    pe.wait_ge(sem.vq, 1)
    pe.wait_ge(sem.oneq, 1)
    for s in (1, 2, 3, 0):
        values(s)

    v.memset(T.m20[:], -20.0).then_inc(sem.m20, 1)
    v.memset(T.ot[:], 1.0).then_inc(sem.one, 1)
    v.wait_ge(sem.one, 1)
    v.quantize_mx(col(T.vc, 1, 128, 0, 128), col(T.vs, 1, 128, 0, 128), T.ot[:]).then_inc(sem.oneq, 1)
    v.wait_ge(sem.dq, 16)
    v.quantize_mx(col(T.qc, me, 128, 0, 128), col(T.qs, me, 128, 0, 128), T.qt[:]).then_inc(sem.qq, 1)
    for h in range(2):
        v.wait_ge(sem["dk%d" % h], 16)
        v.quantize_mx(col(T.kc, h, 256, 0, 256), col(T.ks, h, 256, 0, 256),
                      col(T.kt, h, 1024, 0, 1024)).then_inc(sem.kq, 1)
    max_(0)
    v.wait_ge(sem.dv, 16)
    v.quantize_mx(col(T.vc, 0, 128, 0, 128), col(T.vs, 0, 128, 0, 128), T.vt[:]).then_inc(sem.vq, 1)
    v.wait_ge(sem.fl, 1)
    max_(1)
    for s in (1, 2, 3, 0):
        turn(s)
        if s in (1, 2):
            max_(s + 1)
        place(s)
        v.wait_ge(sem["cl_%d" % s], 1)
        quant(s)
    v.wait_ge(sem.c_0, 1)
    for s in (1, 2):
        v.wait_ge(sem["ar%d" % s], engines(cores[home[s]])[1])
    v.wait_ge(sem.arc, engines(cores[home[3]])[1])
    v.tensor_reduce(T.negm[:], T.land[:, 129:4 * LW:LW], AxisListType.X, AluOpType.max, negate=True).then_inc(sem.negm, 1)
    v.wait_ge(sem.w, 1)
    v.tensor_scalar(T.t2[:], col(T.land, 2, LW, 0, 129), T.w4[:, 2:3], None, AluOpType.mult).then_inc(sem.t2, 1)
    v.wait_ge(sem.t1, 1)
    v.wait_ge(sem.t2, 1)
    v.tensor_tensor(T.acc[:], T.t1[:], T.t2[:], AluOpType.add).then_inc(sem.acc, 1)
    v.wait_ge(sem.t0, 1)
    v.wait_ge(sem.acc, 1)
    v.tensor_tensor(T.acc2[:], T.acc[:], T.t0[:], AluOpType.add).then_inc(sem.acc2, 1)
    v.wait_ge(sem.acc2, 1)
    v.wait_ge(sem.ar3, engines(cores[home[3]])[1])
    v.tensor_scalar(T.den[:], col(T.land, 3, LW, 128, 129), T.w4[:, 3:4], T.acc2[:, 128:129],
                    AluOpType.mult, AluOpType.add).then_inc(sem.den, 1)
    v.wait_ge(sem.den, 1)
    v.reciprocal(T.rec[:], T.den[:]).then_inc(sem.rec, 1)
    v.wait_ge(sem.t3, 1)
    v.tensor_tensor(T.num[:], T.acc2[:, 0:128], T.t3[:], AluOpType.add).then_inc(sem.num, 1)
    v.wait_ge(sem.rec, 1)
    v.wait_ge(sem.num, 1)

    def norm(i, b):
        return (T.y[32 * b:32 * b + 32, 32 * i:32 * i + 32], T.num[32 * i:32 * i + 32, 32 * b:32 * b + 32],
                T.rec[32 * i:32 * i + 32, 0:1])
    for i, b in order[:16 - TAIL]:
        y, num, rec = norm(i, b)
        v.tensor_scalar(y, num, rec, None, AluOpType.mult).then_inc(sem.y, 1)
    v.wait_ge(sem.y, 16)
    v.transpose(T.ox[:], T.y[:]).then_inc(sem.ox, 1)

    a.wait_ge(sem.m20, 1)
    a.activation(T.fl[:], T.m20[:], AF.Exp).then_inc(sem.fl, 1)
    exp_(0)
    shift(0)
    exp_(1)
    half_(2)
    place_act(1)
    exp_(2)
    half_(3)
    shift(1)
    out(1)
    place_act(2)
    exp_(3)
    shift(3)
    shift(2)
    out(2)
    place_act(3)
    out(3)
    place_act(0)
    a.wait_ge(sem.negm, 1)
    a.activation(T.w4[:], T.land[:, 129:4 * LW:LW], AF.Exp, bias=T.negm[:]).then_inc(sem.w, 1)
    a.wait_ge(sem.w, 1)
    a.wait_ge(sem.ar1, engines(cores[home[1]])[1])
    a.activation(T.t1[:], col(T.land, 1, LW, 0, 129), AF.Identity, scale=T.w4[:, 1:2]).then_inc(sem.t1, 1)
    a.wait_ge(sem.a_0, 1)
    a.activation(T.t0[:], bank(0, 0, 0, 129), AF.Identity, scale=T.w4[:, 0:1]).then_inc(sem.t0, 1)
    a.wait_ge(sem.ar3, engines(cores[home[3]])[1])
    a.activation(T.t3[:], col(T.land, 3, LW, 0, 128), AF.Identity, scale=T.w4[:, 3:4]).then_inc(sem.t3, 1)
    a.wait_ge(sem.rec, 1)
    a.wait_ge(sem.num, 1)
    for i, b in order[16 - TAIL:]:
        y, num, rec = norm(i, b)
        a.activation(y, num, AF.Identity, scale=rec).then_inc(sem.y, 1)

    sent = 0
    g.wait_ge(sem.qq, 1)
    qs, qc = col(T.qs, me, 128, 0, 128), col(T.qc, me, 128, 0, 128).bitcast(dt.uint8)

    def send(to, out_ap, in_ap, rsem):
        m, k = engines(to)
        rid, pid, _ = topo.addr(to)
        g.remote_dma(out_ap, in_ap, rsem, sem.sent, pid, rid, m)
        return k

    def result(s, lo, hi, rsem):
        return send(cores[whose[s]], col(T.land, s, LW, lo, hi), col(T.snd, s, LW, lo, hi), rsem)
    for s in (1, 2, 3):
        for part in (qs, qc):
            sent += send(cores[home[s]], part, part, sem["qr%d" % me])
    g.wait_ge(sem.c_1, 1)
    g.wait_ge(sem.out_1, 1)
    sent += result(1, 0, 130, sem.ar1)
    g.wait_ge(sem.c_3, 1)
    sent += result(3, 129, 130, sem.arc)
    g.wait_ge(sem.c_2, 1)
    g.wait_ge(sem.out_2, 1)
    sent += result(2, 0, 130, sem.ar2)
    g.wait_ge(sem.out_3, 1)
    sent += result(3, 0, 129, sem.ar3)
    g.wait_ge(sem.sent, sent)

    stores = 0

    def store(to, what):
        sy.dma_start(to, what).then_inc(sem.st, 16)
        return 16

    def store_c(s):
        sy.wait_ge(sem["c_%d" % s], 1)
        return store(T.c[whose[s]:whose[s] + 1, :], col(T.land if s == 0 else T.snd, s, LW, 129, 130))

    def store_p(s):
        sy.wait_ge(sem["cp_%d" % s], 16)
        return store(T.p[whose[s]], col(T.pt, s, 512, 0, 512))
    stores += store_c(0)
    stores += store_c(1)
    stores += store_p(1)
    stores += store_c(3)
    stores += store_c(2)
    for s in (0, 2, 3):
        stores += store_p(s)
    sy.wait_ge(sem.w, 1)
    for s in range(4):
        stores += store(T.w[home[s]:home[s] + 1, :], T.w4[:, s:s + 1])
    sy.wait_ge(sem.ox, 1)
    stores += store(T.o[:], T.ox[:])
    sy.wait_ge(sem.st, stores)
